import numpy as np
import ml_dtypes


def mxq(x, axis, fmt="e4m3"):
    dtype, down = {"e4m3": (ml_dtypes.float8_e4m3fn, 7), "e5m2": (ml_dtypes.float8_e5m2, 14)}[fmt]
    v = np.moveaxis(np.asarray(x, np.float32).astype(ml_dtypes.bfloat16).astype(np.float64), axis, -1)
    blocks = v.reshape(v.shape[:-1] + (-1, 32))
    amax = np.abs(blocks).max(-1, keepdims=True)
    byte = np.maximum(np.where(amax > 0, np.frexp(amax)[1] - 1 + 127, 0) - down, 1)
    scale = np.exp2(byte - 127.0)
    codes = (blocks / scale).astype(np.float32).astype(dtype).astype(np.float64)
    return np.moveaxis((codes * scale).reshape(v.shape), -1, axis)


WIDE = False


def mx_kscale(k):
    if not WIDE:
        return np.ones(k)
    levels = np.array([30, -30])
    if k % 512:
        return np.exp2(np.random.permutation(np.resize(levels, k // 32))).repeat(32)
    a = np.empty((k // 512, 16))
    for p in range(k // 512):
        a[p, :8] = np.random.permutation(np.resize(levels, 8))
        for g in range(8):
            far = levels[np.abs(levels - a[p, g]) >= 10]
            a[p, g + 8] = far[np.random.randint(len(far))]
    return np.exp2(a.ravel()).repeat(32)


def f64(x):
    return np.asarray(x).astype(np.float64)


def striped(idx):
    return np.tile(np.asarray(idx).reshape(-1, 16).T, (8, 1)).astype(np.uint16)


def unstriped(offs):
    return offs[:16].T.reshape(-1).astype(np.int64)


def striped8(idx):
    return np.asarray(idx).reshape(8, -1, 16).transpose(0, 2, 1).reshape(128, -1).astype(np.uint16)


def unstriped8(offs):
    return offs.reshape(8, 16, -1).transpose(0, 2, 1).reshape(8, -1).astype(np.int64)


def pick8(x, idx, run):
    r = np.arange(len(x))
    return x[r[:, None], idx[r % (8 * run) // run]]


E2M1 = np.array([0.0, 0.5, 1.0, 1.5, 2.0, 3.0, 4.0, 6.0, -0.0, -0.5, -1.0, -1.5, -2.0, -3.0, -4.0, -6.0])


def pack_weight(w, fmt):
    k, n = w.shape
    w = f64(np.asarray(w, np.float32).astype(ml_dtypes.bfloat16)).reshape(k // 32, 32, n)
    amax = np.abs(w).max(1)
    if fmt in ("e4m3", "e5m2"):
        byte = np.frexp(amax)[1] - 1 + 127 - (7 if fmt == "e4m3" else 14)
    else:
        mant, ex = np.frexp(amax / 6.0)
        byte = np.where(mant > 0.5, ex, ex - 1) + 127
    byte = np.clip(np.where(amax > 0, byte, 1), 1, 254)
    scaled = (w * np.exp2(127.0 - byte)[:, None, :]).reshape(k, n).astype(np.float32)
    by_word = np.ascontiguousarray(scaled.reshape(k // 512, 128, 4, n).transpose(0, 1, 3, 2))
    if fmt in ("e4m3", "e5m2"):
        words = by_word.astype(ml_dtypes.float8_e4m3fn if fmt == "e4m3" else ml_dtypes.float8_e5m2).view(np.uint8)
    else:
        c = by_word.astype(ml_dtypes.float4_e2m1fn).view(np.uint8) & 0xF
        words = (c[..., 0::2] | (c[..., 1::2] << 4)).reshape(k // 512, 128, 2 * n)
    return np.ascontiguousarray(words), np.ascontiguousarray(byte.astype(np.uint8).reshape(k // 512, 16, n))


def unpack_weight(words, scales, fmt):
    g, _, n = scales.shape
    words = np.ascontiguousarray(words).reshape(g, 128, n, -1)
    if fmt in ("e4m3", "e5m2"):
        vals = words.view(ml_dtypes.float8_e4m3fn if fmt == "e4m3" else ml_dtypes.float8_e5m2).astype(np.float64)
    else:
        nib = np.empty((g, 128, n, 4), np.uint8)
        nib[..., 0::2] = words & 0xF
        nib[..., 1::2] = words >> 4
        vals = E2M1[nib]
    vals = vals * np.repeat(np.exp2(scales.astype(np.float64) - 127.0), 8, axis=1)[..., None]
    return vals.transpose(0, 1, 3, 2).reshape(g * 512, n)


def sigmoid(v):
    return 1.0 / (1.0 + np.exp(-v))


def sgn(shape):
    return np.random.uniform(0.5, 2.0, shape) * np.where(np.random.standard_normal(shape) < 0, -1.0, 1.0)


K, T, J, R, C, N = 512, 1024, 256, 512, 512, 256


def setup_inputs():
    n = np.random.standard_normal
    idx = np.random.permutation(T)[:J]
    idx2 = np.stack([np.random.permutation(C)[:J] for _ in range(8)])
    idx3 = np.stack([np.random.permutation(C)[:J] for _ in range(8)])
    fk = mx_kscale(K)
    fr = mx_kscale(R)
    xtp = pack_weight(n((K, T)) / fk[:, None], "e2m1")
    wp = pack_weight(n((K, R)) * 1 / np.sqrt(K) * fk[:, None] * fr, "e5m2")
    w2p = pack_weight(n((K, R)) * 1 / np.sqrt(K) * fk[:, None], "e4m3")
    wbp = pack_weight(n((R, N)) * 1 / np.sqrt(R) / fr[:, None], "e4m3")
    return {
        "xt_words": xtp[0],
        "xt_scales": xtp[1],
        "w_words": wp[0],
        "w_scales": wp[1],
        "w2_words": w2p[0],
        "w2_scales": w2p[1],
        "sg": (sgn((R, 1))).astype(np.float32),
        "bg": (np.random.uniform(-2.0, 2.0, (R, 1))).astype(np.float32),
        "wb_words": wbp[0],
        "wb_scales": wbp[1],
        "offs": striped(idx),
        "offs2": striped8(idx2),
        "offs3": striped8(idx3),
    }


def reference(xt_words, xt_scales, w_words, w_scales, w2_words, w2_scales, sg, bg, wb_words, wb_scales, offs, offs2, offs3):
    idx = unstriped(offs)
    idx2 = unstriped8(offs2)
    idx3 = unstriped8(offs3)
    xtu = unpack_weight(xt_words, xt_scales, "e2m1")
    wu = unpack_weight(w_words, w_scales, "e5m2")
    w2u = unpack_weight(w2_words, w2_scales, "e4m3")
    wbu = unpack_weight(wb_words, wb_scales, "e4m3")
    xtidxg = xtu[:, idx]
    a = wu.T @ xtidxg
    b = w2u.T @ xtidxg
    pa = np.zeros((R, C))
    pa[np.arange(R)[:, None], idx2[np.arange(R) % 512 // 64]] = a
    pb = np.zeros((R, C))
    pb[np.arange(R)[:, None], idx3[np.arange(R) % 512 // 64]] = b
    hid = pa * sigmoid(pb * f64(sg) + f64(bg))
    hidq = mxq(hid, 0, "e5m2")
    p = wbu.T @ hidq
    return p

@@ -1,0 +1,209 @@
+from contextlib import ExitStack
+
+import concourse.mybir as mybir
+
+K, T, J, R, C, N = 512, 1024, 256, 512, 512, 256
+FLOPS = 2 * (2 * K * R * J + R * N * C)
+
+F32 = mybir.dt.float32
+BF16 = mybir.dt.bfloat16
+I32 = mybir.dt.int32
+U32 = mybir.dt.uint32
+U16 = mybir.dt.uint16
+U8 = mybir.dt.uint8
+E2M1 = mybir.dt.float4_e2m1fn_x4
+E4M3 = mybir.dt.float8_e4m3fn_x4
+E5M2 = mybir.dt.float8_e5m2_x4
+ACT = mybir.ActivationFunctionType
+ALU = mybir.AluOpType
+
+P = 128
+PACK = 4
+QUADS = 4
+HALF = J // 2
+CHUNK = 128
+CHUNKS = C // CHUNK
+
+
+def tile_list_gatedboards_kernel(
+    tc, xt_words, xt_scales, w_words, w_scales, w2_words, w2_scales, sg, bg, wb_words, wb_scales, offs, offs2, offs3, out
+):
+    nc = tc.nc
+    with ExitStack() as ctx:
+        keep = ctx.enter_context(tc.tile_pool(name="keep", bufs=1))
+        boards = ctx.enter_context(tc.tile_pool(name="boards", bufs=PACK))
+        psum = ctx.enter_context(tc.psum_pool(name="psum", bufs=1))
+
+        def words_of(packed):
+            return packed[0].rearrange("p n t -> p (n t)").bitcast(I32)
+
+        def load_scale_rows(plane, scales, queue):
+            nc.vector.memset(plane[:].bitcast(I32), 0)
+            for q in range(QUADS):
+                queue.dma_start(plane[32 * q : 32 * q + 4, :].bitcast(I32), scales[0, 4 * q : 4 * q + 4, :].bitcast(I32))
+
+        def stage_scale_rows(name, scales):
+            staged = keep.tile([4, QUADS, R // 4], I32, name=name)
+            nc.sync.dma_start(staged[:], scales[0].rearrange("(q i) n -> i q n", i=4).bitcast(I32))
+            return staged
+
+        def spread_scale_rows(name, staged):
+            plane = keep.tile([P, R], U8, name=name, align_bytes=64)
+            nc.vector.memset(plane[:].bitcast(I32), 0)
+            for q in range(QUADS):
+                nc.vector.tensor_copy(plane[32 * q : 32 * q + 4, :].bitcast(I32), staged[:, q, :])
+            return plane
+
+        w2_staged = stage_scale_rows("w2_staged", w2_scales)
+        token_list = keep.tile([P, J // 16], U16)
+        nc.sync.dma_start(token_list[:], offs)
+        xt_word_table = keep.tile([P, T], U16, align_bytes=64)
+        nc.sync.dma_start(xt_word_table[:].bitcast(I32), xt_words[0].bitcast(I32))
+        xt_scale_table = keep.tile([P, T], U8, align_bytes=64)
+        load_scale_rows(xt_scale_table, xt_scales, nc.sync)
+        w2_loaded = keep.tile([P, R], I32)
+        nc.sync.dma_start(w2_loaded[:], words_of(w2_words))
+        b_lists = keep.tile([P, J // 16], U16)
+        nc.sync.dma_start(b_lists[:], offs3)
+        slope = keep.tile([P, PACK], F32)
+        nc.sync.dma_start(slope[:], sg.rearrange("(p t) o -> p (t o)", t=PACK))
+        offset = keep.tile([P, PACK], F32)
+        nc.sync.dma_start(offset[:], bg.rearrange("(p t) o -> p (t o)", t=PACK))
+        w_raw = keep.tile([P, R], U8, align_bytes=64)
+        load_scale_rows(w_raw, w_scales, nc.sync)
+        w_loaded = keep.tile([P, R], I32)
+        nc.sync.dma_start(w_loaded[:], words_of(w_words))
+        a_lists = keep.tile([P, J // 16], U16)
+        nc.sync.dma_start(a_lists[:], offs2)
+        wb_codes = keep.tile([P, N], I32, align_bytes=64)
+        nc.sync.dma_start(wb_codes[:], words_of(wb_words))
+        wb_plane = keep.tile([P, N], U8, align_bytes=64)
+        load_scale_rows(wb_plane, wb_scales, nc.sync)
+
+        x_codes = [keep.tile([P, HALF], U16, name="x_codes%d" % h, align_bytes=64) for h in range(2)]
+        x_plane = [keep.tile([P, HALF], U8, name="x_plane%d" % h, align_bytes=64) for h in range(2)]
+        w2_raw = spread_scale_rows("w2_raw", w2_staged)
+        w2_codes = keep.tile([P, PACK, P], U32, tag="dealt_codes", align_bytes=64)
+        w2_plane = keep.tile([P, PACK, P], U8, tag="dealt_plane", align_bytes=64)
+        w2_dealt = w2_loaded[:].bitcast(U32).rearrange("p (m t) -> p t m", t=PACK)
+        nc.scalar.copy(w2_codes[:, 0, :], w2_dealt[:, 0, :])
+        nc.scalar.copy(w2_codes[:, 1:, :], w2_dealt[:, 1:, :])
+        nc.vector.tensor_copy(w2_plane[:, 0, :], w2_raw[:, 0:R:PACK])
+
+        def gather(h):
+            picks = token_list[:, h * HALF // 16 : (h + 1) * HALF // 16]
+            nc.vector.tensor_copy(x_codes[h][:], xt_word_table[:].indirect(picks))
+            nc.vector.tensor_copy(x_plane[h][:], xt_scale_table[:].indirect(picks))
+
+        def first_stage(name, codes, plane, fmt, t, halves):
+            acc = psum.tile([P, len(halves), HALF], F32, name="acc", tag="acc", bufs=6)
+            for i, h in enumerate(halves):
+                nc.tensor.matmul_mx(
+                    out=acc[:, i, :],
+                    lhsT=codes[:, t, :].bitcast(fmt),
+                    lhsT_scale=plane[:, t, :],
+                    rhs=x_codes[h][:].bitcast(E2M1),
+                    rhs_scale=x_plane[h][:],
+                    start=True,
+                    stop=True,
+                )
+            result = keep.tile([P, len(halves) * HALF], F32, name=name)
+            nc.vector.tensor_copy(result[:], acc[:].rearrange("p h j -> p (h j)"))
+            return result
+
+        every = slice(0, J)
+        b_parts = []
+        for h in range(2):
+            gather(h)
+            b_parts.append((0, slice(h * HALF, (h + 1) * HALF), first_stage("b0_%d" % h, w2_codes, w2_plane, E4M3, 0, [h])))
+        nc.vector.tensor_copy(w2_plane[:, 1:, :], w2_raw[:].rearrange("p (m t) -> p t m", t=PACK)[:, 1:, :])
+        for t in range(1, PACK):
+            b_parts.append((t, every, first_stage("b%d" % t, w2_codes, w2_plane, E4M3, t, [0, 1])))
+
+        w_codes = keep.tile([P, PACK, P], I32, tag="dealt_codes", align_bytes=64)
+        w_plane = keep.tile([P, PACK, P], U8, tag="dealt_plane", align_bytes=64)
+        nc.vector.tensor_copy(w_codes[:], w_loaded[:].rearrange("p (m t) -> p t m", t=PACK))
+        nc.vector.tensor_copy(w_plane[:], w_raw[:].rearrange("p (m t) -> p t m", t=PACK))
+        a_parts = [first_stage("a%d" % t, w_codes, w_plane, E5M2, t, [0, 1]) for t in range(PACK)]
+
+        half_slope = keep.tile([P, PACK], F32)
+        half_offset = keep.tile([P, PACK], F32)
+        nc.gpsimd.tensor_scalar(half_slope[:], slope[:], 0.5, 0.0, ALU.mult, ALU.add)
+        nc.gpsimd.tensor_scalar(half_offset[:], offset[:], 0.5, 0.0, ALU.mult, ALU.add)
+
+        def new_board(engine):
+            board = boards.tile([P, C], F32, name="board")
+            engine.memset(board[:], 0.0)
+            return board
+
+        def scatter(board, lists, cols, values):
+            places = lists[:, cols.start // 16 : cols.stop // 16]
+            nc.scalar.activation(board[:].indirect(places), values[:], ACT.Copy)
+
+        pb = [new_board(nc.gpsimd) for t in range(PACK)]
+        pa = []
+        gates = []
+
+        def make_gate(t):
+            th = keep.tile([P, C], F32, name="tanh%d" % t)
+            nc.scalar.activation(th[:], pb[t][:], ACT.Tanh, bias=half_offset[:, t : t + 1], scale=half_slope[:, t : t + 1])
+            pa.append(new_board(nc.gpsimd))
+            gate = keep.tile([P, C], F32, name="gate%d" % t)
+            nc.gpsimd.tensor_scalar(gate[:], th[:], 0.5, 0.5, ALU.mult, ALU.add)
+            gates.append(gate)
+
+        for t, cols, values in b_parts:
+            scatter(pb[t], b_lists, cols, values)
+            if t > 0:
+                make_gate(t - 1)
+        make_gate(PACK - 1)
+
+        rounded = [keep.tile([P, PACK, C // 2], BF16, name="rounded%d" % h) for h in range(2)]
+        hid = [keep.tile([P, CHUNK, PACK], BF16, name="hid%d" % i, align_bytes=64) for i in range(CHUNKS)]
+        out_rows = out.rearrange("(g p) c -> p g c", p=P)
+
+        def weave(i, t):
+            h, at = divmod(i * CHUNK, C // 2)
+            pair = rounded[h][:, t : t + 2, at : at + CHUNK]
+            nc.vector.tensor_copy(hid[i][:, :, t : t + 2], pair.rearrange("p t c -> p c t"))
+
+        def second_stage(i):
+            codes = keep.tile([P, CHUNK], U32, name="hid_codes%d" % i, align_bytes=64)
+            plane = keep.tile([P, CHUNK], U8, name="hid_plane%d" % i, align_bytes=64)
+            nc.vector.quantize_mx(out=codes[:].bitcast(E5M2), scales=plane[:], in_=hid[i][:].rearrange("p c t -> p (c t)"))
+            result = keep.tile([P, N // P, CHUNK], F32, name="result%d" % i)
+            last = i == CHUNKS - 1
+            shared = None if last else psum.tile([P, N // P, CHUNK], F32, name="acc", tag="acc", bufs=6)
+            for g in range(N // P):
+                rows = slice(g * P, (g + 1) * P)
+                acc = psum.tile([P, CHUNK], F32, name="acc", tag="acc", bufs=6)[:] if last else shared[:, g, :]
+                nc.tensor.matmul_mx(
+                    out=acc,
+                    lhsT=wb_codes[:, rows].bitcast(E4M3),
+                    lhsT_scale=wb_plane[:, rows],
+                    rhs=codes[:].bitcast(E5M2),
+                    rhs_scale=plane[:],
+                    start=True,
+                    stop=True,
+                )
+                if last and g == 0:
+                    nc.scalar.copy(result[:, g, :], acc)
+                elif last:
+                    nc.vector.tensor_copy(result[:, g, :], acc)
+            if not last:
+                nc.scalar.copy(result[:], shared[:])
+            nc.sync.dma_start(out_rows[:, :, i * CHUNK : (i + 1) * CHUNK], result[:])
+
+        for t in range(PACK):
+            scatter(pa[t], a_lists, every, a_parts[t])
+            for h in range(2):
+                cols = slice(h * C // 2, (h + 1) * C // 2)
+                nc.vector.tensor_tensor(rounded[h][:, t, :], pa[t][:, cols], gates[t][:, cols], ALU.mult)
+            if t == 1:
+                for i in range(CHUNKS):
+                    weave(i, 0)
+        for i in range(CHUNKS + 1):
+            if i < CHUNKS:
+                weave(i, 2)
+            if i > 0:
+                second_stage(i - 1)

@@ -31,7 +31,7 @@ def tile_list_gatedboards_kernel(
     nc = tc.nc
     with ExitStack() as ctx:
         keep = ctx.enter_context(tc.tile_pool(name="keep", bufs=1))
-        boards = ctx.enter_context(tc.tile_pool(name="boards", bufs=PACK))
+        boards = ctx.enter_context(tc.tile_pool(name="boards", bufs=1))
         psum = ctx.enter_context(tc.psum_pool(name="psum", bufs=1))
 
         def words_of(packed):
@@ -48,7 +48,7 @@ def tile_list_gatedboards_kernel(
             return staged
 
         def spread_scale_rows(name, staged):
-            plane = keep.tile([P, R], U8, name=name, align_bytes=64)
+            plane = boards.tile([P, R], U8, name=name, tag="slot3")
             nc.vector.memset(plane[:].bitcast(I32), 0)
             for q in range(QUADS):
                 nc.vector.tensor_copy(plane[32 * q : 32 * q + 4, :].bitcast(I32), staged[:, q, :])
@@ -57,7 +57,7 @@ def tile_list_gatedboards_kernel(
         w2_staged = stage_scale_rows("w2_staged", w2_scales)
         token_list = keep.tile([P, J // 16], U16)
         nc.sync.dma_start(token_list[:], offs)
-        xt_word_table = keep.tile([P, T], U16, align_bytes=64)
+        xt_word_table = boards.tile([P, T], U16, tag="slot2")
         nc.sync.dma_start(xt_word_table[:].bitcast(I32), xt_words[0].bitcast(I32))
         xt_scale_table = keep.tile([P, T], U8, align_bytes=64)
         load_scale_rows(xt_scale_table, xt_scales, nc.sync)
@@ -65,14 +65,14 @@ def tile_list_gatedboards_kernel(
         nc.sync.dma_start(w2_loaded[:], words_of(w2_words))
         b_lists = keep.tile([P, J // 16], U16)
         nc.sync.dma_start(b_lists[:], offs3)
-        slope = keep.tile([P, PACK], F32)
-        nc.sync.dma_start(slope[:], sg.rearrange("(p t) o -> p (t o)", t=PACK))
-        offset = keep.tile([P, PACK], F32)
-        nc.sync.dma_start(offset[:], bg.rearrange("(p t) o -> p (t o)", t=PACK))
         w_raw = keep.tile([P, R], U8, align_bytes=64)
         load_scale_rows(w_raw, w_scales, nc.sync)
         w_loaded = keep.tile([P, R], I32)
         nc.sync.dma_start(w_loaded[:], words_of(w_words))
+        slope = keep.tile([P, PACK], F32)
+        nc.sync.dma_start(slope[:], sg.rearrange("(p t) o -> p (t o)", t=PACK))
+        offset = keep.tile([P, PACK], F32)
+        nc.sync.dma_start(offset[:], bg.rearrange("(p t) o -> p (t o)", t=PACK))
         a_lists = keep.tile([P, J // 16], U16)
         nc.sync.dma_start(a_lists[:], offs2)
         wb_codes = keep.tile([P, N], I32, align_bytes=64)
@@ -112,12 +112,17 @@ def tile_list_gatedboards_kernel(
             return result
 
         every = slice(0, J)
+        w2_bytes = w2_raw[:].rearrange("p (m t) -> p t m", t=PACK)
         b_parts = []
         for h in range(2):
             gather(h)
-            b_parts.append((0, slice(h * HALF, (h + 1) * HALF), first_stage("b0_%d" % h, w2_codes, w2_plane, E4M3, 0, [h])))
-        nc.vector.tensor_copy(w2_plane[:, 1:, :], w2_raw[:].rearrange("p (m t) -> p t m", t=PACK)[:, 1:, :])
-        for t in range(1, PACK):
+            if h == 0:
+                nc.vector.tensor_copy(w2_plane[:, 1, :], w2_bytes[:, 1, :])
+            for t in range(2):
+                values = first_stage("b%d_%d" % (t, h), w2_codes, w2_plane, E4M3, t, [h])
+                b_parts.append((t, slice(h * HALF, (h + 1) * HALF), values))
+        nc.vector.tensor_copy(w2_plane[:, 2:, :], w2_bytes[:, 2:, :])
+        for t in range(2, PACK):
             b_parts.append((t, every, first_stage("b%d" % t, w2_codes, w2_plane, E4M3, t, [0, 1])))
 
         w_codes = keep.tile([P, PACK, P], I32, tag="dealt_codes", align_bytes=64)
@@ -131,8 +136,8 @@ def tile_list_gatedboards_kernel(
         nc.gpsimd.tensor_scalar(half_slope[:], slope[:], 0.5, 0.0, ALU.mult, ALU.add)
         nc.gpsimd.tensor_scalar(half_offset[:], offset[:], 0.5, 0.0, ALU.mult, ALU.add)
 
-        def new_board(engine):
-            board = boards.tile([P, C], F32, name="board")
+        def new_board(t, engine):
+            board = boards.tile([P, C], F32, name="board", tag="slot%d" % t)
             engine.memset(board[:], 0.0)
             return board
 
@@ -140,21 +145,21 @@ def tile_list_gatedboards_kernel(
             places = lists[:, cols.start // 16 : cols.stop // 16]
             nc.scalar.activation(board[:].indirect(places), values[:], ACT.Copy)
 
-        pb = [new_board(nc.gpsimd) for t in range(PACK)]
+        pb = [new_board(t, nc.vector if t < 2 else nc.gpsimd) for t in range(PACK)]
         pa = []
         gates = []
 
         def make_gate(t):
             th = keep.tile([P, C], F32, name="tanh%d" % t)
             nc.scalar.activation(th[:], pb[t][:], ACT.Tanh, bias=half_offset[:, t : t + 1], scale=half_slope[:, t : t + 1])
-            pa.append(new_board(nc.gpsimd))
+            pa.append(new_board(t, nc.gpsimd))
             gate = keep.tile([P, C], F32, name="gate%d" % t)
             nc.gpsimd.tensor_scalar(gate[:], th[:], 0.5, 0.5, ALU.mult, ALU.add)
             gates.append(gate)
 
         for t, cols, values in b_parts:
             scatter(pb[t], b_lists, cols, values)
-            if t > 0:
+            if t > 0 and cols.stop == J:
                 make_gate(t - 1)
         make_gate(PACK - 1)
 

@@ -31,7 +31,6 @@ def tile_list_gatedboards_kernel(
     nc = tc.nc
     with ExitStack() as ctx:
         keep = ctx.enter_context(tc.tile_pool(name="keep", bufs=1))
-        boards = ctx.enter_context(tc.tile_pool(name="boards", bufs=1))
         psum = ctx.enter_context(tc.psum_pool(name="psum", bufs=1))
 
         def words_of(packed):
@@ -48,7 +47,7 @@ def tile_list_gatedboards_kernel(
             return staged
 
         def spread_scale_rows(name, staged):
-            plane = boards.tile([P, R], U8, name=name, tag="slot3")
+            plane = keep.tile([P, R], U8, name=name, align_bytes=64)
             nc.vector.memset(plane[:].bitcast(I32), 0)
             for q in range(QUADS):
                 nc.vector.tensor_copy(plane[32 * q : 32 * q + 4, :].bitcast(I32), staged[:, q, :])
@@ -57,22 +56,22 @@ def tile_list_gatedboards_kernel(
         w2_staged = stage_scale_rows("w2_staged", w2_scales)
         token_list = keep.tile([P, J // 16], U16)
         nc.sync.dma_start(token_list[:], offs)
-        xt_word_table = boards.tile([P, T], U16, tag="slot2")
+        xt_word_table = keep.tile([P, T], U16, align_bytes=64)
         nc.sync.dma_start(xt_word_table[:].bitcast(I32), xt_words[0].bitcast(I32))
-        xt_scale_table = keep.tile([P, T], U8, align_bytes=64)
+        xt_scale_table = keep.tile([P, T], U8, tag="xt_scales", align_bytes=64)
         load_scale_rows(xt_scale_table, xt_scales, nc.sync)
         w2_loaded = keep.tile([P, R], I32)
         nc.sync.dma_start(w2_loaded[:], words_of(w2_words))
         b_lists = keep.tile([P, J // 16], U16)
         nc.sync.dma_start(b_lists[:], offs3)
-        w_raw = keep.tile([P, R], U8, align_bytes=64)
-        load_scale_rows(w_raw, w_scales, nc.sync)
-        w_loaded = keep.tile([P, R], I32)
-        nc.sync.dma_start(w_loaded[:], words_of(w_words))
         slope = keep.tile([P, PACK], F32)
         nc.sync.dma_start(slope[:], sg.rearrange("(p t) o -> p (t o)", t=PACK))
         offset = keep.tile([P, PACK], F32)
         nc.sync.dma_start(offset[:], bg.rearrange("(p t) o -> p (t o)", t=PACK))
+        w_raw = keep.tile([P, R], U8, tag="w_raw", align_bytes=64)
+        load_scale_rows(w_raw, w_scales, nc.sync)
+        w_loaded = keep.tile([P, R], I32, tag="w_loaded", align_bytes=64)
+        nc.sync.dma_start(w_loaded[:], words_of(w_words))
         a_lists = keep.tile([P, J // 16], U16)
         nc.sync.dma_start(a_lists[:], offs2)
         wb_codes = keep.tile([P, N], I32, align_bytes=64)
@@ -136,8 +135,8 @@ def tile_list_gatedboards_kernel(
         nc.gpsimd.tensor_scalar(half_slope[:], slope[:], 0.5, 0.0, ALU.mult, ALU.add)
         nc.gpsimd.tensor_scalar(half_offset[:], offset[:], 0.5, 0.0, ALU.mult, ALU.add)
 
-        def new_board(t, engine):
-            board = boards.tile([P, C], F32, name="board", tag="slot%d" % t)
+        def new_board(tag, engine):
+            board = keep.tile([P, C], F32, name="board", tag=tag, align_bytes=64)
             engine.memset(board[:], 0.0)
             return board
 
@@ -145,14 +144,16 @@ def tile_list_gatedboards_kernel(
             places = lists[:, cols.start // 16 : cols.stop // 16]
             nc.scalar.activation(board[:].indirect(places), values[:], ACT.Copy)
 
-        pb = [new_board(t, nc.vector if t < 2 else nc.gpsimd) for t in range(PACK)]
-        pa = []
+        pb = [new_board(tag, nc.vector) for tag in ("pb0", "pb1")]
+        pb += [new_board(tag, nc.gpsimd) for tag in ("xt_scales", "w_raw")]
+        pa = [new_board(tag, nc.vector) for tag in ("w_loaded", "dealt_codes")]
         gates = []
 
         def make_gate(t):
             th = keep.tile([P, C], F32, name="tanh%d" % t)
             nc.scalar.activation(th[:], pb[t][:], ACT.Tanh, bias=half_offset[:, t : t + 1], scale=half_slope[:, t : t + 1])
-            pa.append(new_board(t, nc.gpsimd))
+            if t < 2:
+                pa.append(new_board("pb%d" % t, nc.gpsimd))
             gate = keep.tile([P, C], F32, name="gate%d" % t)
             nc.gpsimd.tensor_scalar(gate[:], th[:], 0.5, 0.5, ALU.mult, ALU.add)
             gates.append(gate)
@@ -167,10 +168,10 @@ def tile_list_gatedboards_kernel(
         hid = [keep.tile([P, CHUNK, PACK], BF16, name="hid%d" % i, align_bytes=64) for i in range(CHUNKS)]
         out_rows = out.rearrange("(g p) c -> p g c", p=P)
 
-        def weave(i, t):
+        def weave(i, t, copy):
             h, at = divmod(i * CHUNK, C // 2)
             pair = rounded[h][:, t : t + 2, at : at + CHUNK]
-            nc.vector.tensor_copy(hid[i][:, :, t : t + 2], pair.rearrange("p t c -> p c t"))
+            copy(hid[i][:, :, t : t + 2], pair.rearrange("p t c -> p c t"))
 
         def second_stage(i):
             codes = keep.tile([P, CHUNK], U32, name="hid_codes%d" % i, align_bytes=64)
@@ -206,9 +207,9 @@ def tile_list_gatedboards_kernel(
                 nc.vector.tensor_tensor(rounded[h][:, t, :], pa[t][:, cols], gates[t][:, cols], ALU.mult)
             if t == 1:
                 for i in range(CHUNKS):
-                    weave(i, 0)
+                    weave(i, 0, nc.vector.tensor_copy)
         for i in range(CHUNKS + 1):
             if i < CHUNKS:
-                weave(i, 2)
+                weave(i, 2, nc.scalar.copy if i % 2 else nc.vector.tensor_copy)
             if i > 0:
                 second_stage(i - 1)

@@ -79,7 +79,7 @@ def tile_list_gatedboards_kernel(
         wb_plane = keep.tile([P, N], U8, align_bytes=64)
         load_scale_rows(wb_plane, wb_scales, nc.sync)
 
-        x_codes = [keep.tile([P, HALF], U16, name="x_codes%d" % h, align_bytes=64) for h in range(2)]
+        x_codes = [keep.tile([P, HALF], U16, name="x_codes%d" % h, tag="x_codes%d" % h, align_bytes=64) for h in range(2)]
         x_plane = [keep.tile([P, HALF], U8, name="x_plane%d" % h, align_bytes=64) for h in range(2)]
         w2_raw = spread_scale_rows("w2_raw", w2_staged)
         w2_codes = keep.tile([P, PACK, P], U32, tag="dealt_codes", align_bytes=64)
@@ -147,16 +147,14 @@ def tile_list_gatedboards_kernel(
         pb = [new_board(tag, nc.vector) for tag in ("pb0", "pb1")]
         pb += [new_board(tag, nc.gpsimd) for tag in ("xt_scales", "w_raw")]
         pa = [new_board(tag, nc.vector) for tag in ("w_loaded", "dealt_codes")]
-        gates = []
+        gates = keep.tile([P, PACK, C], F32, tag="x_codes1", align_bytes=64)
 
         def make_gate(t):
             th = keep.tile([P, C], F32, name="tanh%d" % t)
             nc.scalar.activation(th[:], pb[t][:], ACT.Tanh, bias=half_offset[:, t : t + 1], scale=half_slope[:, t : t + 1])
             if t < 2:
                 pa.append(new_board("pb%d" % t, nc.gpsimd))
-            gate = keep.tile([P, C], F32, name="gate%d" % t)
-            nc.gpsimd.tensor_scalar(gate[:], th[:], 0.5, 0.5, ALU.mult, ALU.add)
-            gates.append(gate)
+            nc.vector.tensor_scalar(gates[:, t, :], th[:], 0.5, 0.5, ALU.mult, ALU.add)
 
         for t, cols, values in b_parts:
             scatter(pb[t], b_lists, cols, values)
@@ -204,7 +202,7 @@ def tile_list_gatedboards_kernel(
             scatter(pa[t], a_lists, every, a_parts[t])
             for h in range(2):
                 cols = slice(h * C // 2, (h + 1) * C // 2)
-                nc.vector.tensor_tensor(rounded[h][:, t, :], pa[t][:, cols], gates[t][:, cols], ALU.mult)
+                nc.vector.tensor_tensor(rounded[h][:, t, :], pa[t][:, cols], gates[:, t, cols], ALU.mult)
             if t == 1:
                 for i in range(CHUNKS):
                     weave(i, 0, nc.vector.tensor_copy)

from contextlib import ExitStack

import concourse.mybir as mybir

K, T, J, R, C, N = 512, 1024, 256, 512, 512, 256
FLOPS = 2 * (2 * K * R * J + R * N * C)

F32 = mybir.dt.float32
BF16 = mybir.dt.bfloat16
I32 = mybir.dt.int32
U32 = mybir.dt.uint32
U16 = mybir.dt.uint16
U8 = mybir.dt.uint8
E2M1 = mybir.dt.float4_e2m1fn_x4
E4M3 = mybir.dt.float8_e4m3fn_x4
E5M2 = mybir.dt.float8_e5m2_x4
ACT = mybir.ActivationFunctionType
ALU = mybir.AluOpType

P = 128
PACK = 4
QUADS = 4
HALF = J // 2
CHUNK = 128
CHUNKS = C // CHUNK


def tile_list_gatedboards_kernel(
    tc, xt_words, xt_scales, w_words, w_scales, w2_words, w2_scales, sg, bg, wb_words, wb_scales, offs, offs2, offs3, out
):
    nc = tc.nc
    with ExitStack() as ctx:
        keep = ctx.enter_context(tc.tile_pool(name="keep", bufs=1))
        psum = ctx.enter_context(tc.psum_pool(name="psum", bufs=1))

        def words_of(packed):
            return packed[0].rearrange("p n t -> p (n t)").bitcast(I32)

        def load_scale_rows(plane, scales, queue):
            nc.vector.memset(plane[:].bitcast(I32), 0)
            for q in range(QUADS):
                queue.dma_start(plane[32 * q : 32 * q + 4, :].bitcast(I32), scales[0, 4 * q : 4 * q + 4, :].bitcast(I32))

        def stage_scale_rows(name, scales):
            staged = keep.tile([4, QUADS, R // 4], I32, name=name)
            nc.sync.dma_start(staged[:], scales[0].rearrange("(q i) n -> i q n", i=4).bitcast(I32))
            return staged

        def spread_scale_rows(name, staged):
            plane = keep.tile([P, R], U8, name=name, align_bytes=64)
            nc.vector.memset(plane[:].bitcast(I32), 0)
            for q in range(QUADS):
                nc.vector.tensor_copy(plane[32 * q : 32 * q + 4, :].bitcast(I32), staged[:, q, :])
            return plane

        w2_staged = stage_scale_rows("w2_staged", w2_scales)
        token_list = keep.tile([P, J // 16], U16)
        nc.sync.dma_start(token_list[:], offs)
        xt_word_table = keep.tile([P, T], U16, align_bytes=64)
        nc.sync.dma_start(xt_word_table[:].bitcast(I32), xt_words[0].bitcast(I32))
        xt_scale_table = keep.tile([P, T], U8, tag="xt_scales", align_bytes=64)
        load_scale_rows(xt_scale_table, xt_scales, nc.sync)
        w2_loaded = keep.tile([P, R], I32)
        nc.sync.dma_start(w2_loaded[:], words_of(w2_words))
        b_lists = keep.tile([P, J // 16], U16)
        nc.sync.dma_start(b_lists[:], offs3)
        slope = keep.tile([P, PACK], F32)
        nc.sync.dma_start(slope[:], sg.rearrange("(p t) o -> p (t o)", t=PACK))
        offset = keep.tile([P, PACK], F32)
        nc.sync.dma_start(offset[:], bg.rearrange("(p t) o -> p (t o)", t=PACK))
        w_raw = keep.tile([P, R], U8, tag="w_raw", align_bytes=64)
        load_scale_rows(w_raw, w_scales, nc.sync)
        w_loaded = keep.tile([P, R], I32, tag="w_loaded", align_bytes=64)
        nc.sync.dma_start(w_loaded[:], words_of(w_words))
        a_lists = keep.tile([P, J // 16], U16)
        nc.sync.dma_start(a_lists[:], offs2)
        wb_codes = keep.tile([P, N], I32, align_bytes=64)
        nc.sync.dma_start(wb_codes[:], words_of(wb_words))
        wb_plane = keep.tile([P, N], U8, align_bytes=64)
        load_scale_rows(wb_plane, wb_scales, nc.sync)

        x_codes = [keep.tile([P, HALF], U16, name="x_codes%d" % h, tag="x_codes%d" % h, align_bytes=64) for h in range(2)]
        x_plane = [keep.tile([P, HALF], U8, name="x_plane%d" % h, align_bytes=64) for h in range(2)]
        w2_raw = spread_scale_rows("w2_raw", w2_staged)
        w2_codes = keep.tile([P, PACK, P], U32, tag="dealt_codes", align_bytes=64)
        w2_plane = keep.tile([P, PACK, P], U8, tag="dealt_plane", align_bytes=64)
        w2_dealt = w2_loaded[:].bitcast(U32).rearrange("p (m t) -> p t m", t=PACK)
        nc.scalar.copy(w2_codes[:, 0, :], w2_dealt[:, 0, :])
        nc.scalar.copy(w2_codes[:, 1:, :], w2_dealt[:, 1:, :])
        nc.vector.tensor_copy(w2_plane[:, 0, :], w2_raw[:, 0:R:PACK])

        def gather(h):
            picks = token_list[:, h * HALF // 16 : (h + 1) * HALF // 16]
            nc.vector.tensor_copy(x_codes[h][:], xt_word_table[:].indirect(picks))
            nc.vector.tensor_copy(x_plane[h][:], xt_scale_table[:].indirect(picks))

        def first_stage(name, codes, plane, fmt, t, halves):
            acc = psum.tile([P, len(halves), HALF], F32, name="acc", tag="acc", bufs=6)
            for i, h in enumerate(halves):
                nc.tensor.matmul_mx(
                    out=acc[:, i, :],
                    lhsT=codes[:, t, :].bitcast(fmt),
                    lhsT_scale=plane[:, t, :],
                    rhs=x_codes[h][:].bitcast(E2M1),
                    rhs_scale=x_plane[h][:],
                    start=True,
                    stop=True,
                )
            result = keep.tile([P, len(halves) * HALF], F32, name=name)
            nc.vector.tensor_copy(result[:], acc[:].rearrange("p h j -> p (h j)"))
            return result

        every = slice(0, J)
        w2_bytes = w2_raw[:].rearrange("p (m t) -> p t m", t=PACK)
        b_parts = []
        for h in range(2):
            gather(h)
            if h == 0:
                nc.vector.tensor_copy(w2_plane[:, 1, :], w2_bytes[:, 1, :])
            for t in range(2):
                values = first_stage("b%d_%d" % (t, h), w2_codes, w2_plane, E4M3, t, [h])
                b_parts.append((t, slice(h * HALF, (h + 1) * HALF), values))
        nc.vector.tensor_copy(w2_plane[:, 2:, :], w2_bytes[:, 2:, :])
        for t in range(2, PACK):
            b_parts.append((t, every, first_stage("b%d" % t, w2_codes, w2_plane, E4M3, t, [0, 1])))

        w_codes = keep.tile([P, PACK, P], I32, tag="dealt_codes", align_bytes=64)
        w_plane = keep.tile([P, PACK, P], U8, tag="dealt_plane", align_bytes=64)
        nc.vector.tensor_copy(w_codes[:], w_loaded[:].rearrange("p (m t) -> p t m", t=PACK))
        nc.vector.tensor_copy(w_plane[:], w_raw[:].rearrange("p (m t) -> p t m", t=PACK))
        a_parts = [first_stage("a%d" % t, w_codes, w_plane, E5M2, t, [0, 1]) for t in range(PACK)]

        half_slope = keep.tile([P, PACK], F32)
        half_offset = keep.tile([P, PACK], F32)
        nc.gpsimd.tensor_scalar(half_slope[:], slope[:], 0.5, 0.0, ALU.mult, ALU.add)
        nc.gpsimd.tensor_scalar(half_offset[:], offset[:], 0.5, 0.0, ALU.mult, ALU.add)

        def new_board(tag, engine):
            board = keep.tile([P, C], F32, name="board", tag=tag, align_bytes=64)
            engine.memset(board[:], 0.0)
            return board

        def scatter(board, lists, cols, values):
            places = lists[:, cols.start // 16 : cols.stop // 16]
            nc.scalar.activation(board[:].indirect(places), values[:], ACT.Copy)

        pb = [new_board(tag, nc.vector) for tag in ("pb0", "pb1")]
        pb += [new_board(tag, nc.gpsimd) for tag in ("xt_scales", "w_raw")]
        pa = [new_board(tag, nc.vector) for tag in ("w_loaded", "dealt_codes")]
        gates = keep.tile([P, PACK, C], F32, tag="x_codes1", align_bytes=64)

        def make_gate(t):
            th = keep.tile([P, C], F32, name="tanh%d" % t)
            nc.scalar.activation(th[:], pb[t][:], ACT.Tanh, bias=half_offset[:, t : t + 1], scale=half_slope[:, t : t + 1])
            if t < 2:
                pa.append(new_board("pb%d" % t, nc.gpsimd))
            nc.vector.tensor_scalar(gates[:, t, :], th[:], 0.5, 0.5, ALU.mult, ALU.add)

        for t, cols, values in b_parts:
            scatter(pb[t], b_lists, cols, values)
            if t > 0 and cols.stop == J:
                make_gate(t - 1)
        make_gate(PACK - 1)

        rounded = [keep.tile([P, PACK, C // 2], BF16, name="rounded%d" % h) for h in range(2)]
        hid = [keep.tile([P, CHUNK, PACK], BF16, name="hid%d" % i, align_bytes=64) for i in range(CHUNKS)]
        out_rows = out.rearrange("(g p) c -> p g c", p=P)

        def weave(i, t, copy):
            h, at = divmod(i * CHUNK, C // 2)
            pair = rounded[h][:, t : t + 2, at : at + CHUNK]
            copy(hid[i][:, :, t : t + 2], pair.rearrange("p t c -> p c t"))

        def second_stage(i):
            codes = keep.tile([P, CHUNK], U32, name="hid_codes%d" % i, align_bytes=64)
            plane = keep.tile([P, CHUNK], U8, name="hid_plane%d" % i, align_bytes=64)
            nc.vector.quantize_mx(out=codes[:].bitcast(E5M2), scales=plane[:], in_=hid[i][:].rearrange("p c t -> p (c t)"))
            result = keep.tile([P, N // P, CHUNK], F32, name="result%d" % i)
            last = i == CHUNKS - 1
            shared = None if last else psum.tile([P, N // P, CHUNK], F32, name="acc", tag="acc", bufs=6)
            for g in range(N // P):
                rows = slice(g * P, (g + 1) * P)
                acc = psum.tile([P, CHUNK], F32, name="acc", tag="acc", bufs=6)[:] if last else shared[:, g, :]
                nc.tensor.matmul_mx(
                    out=acc,
                    lhsT=wb_codes[:, rows].bitcast(E4M3),
                    lhsT_scale=wb_plane[:, rows],
                    rhs=codes[:].bitcast(E5M2),
                    rhs_scale=plane[:],
                    start=True,
                    stop=True,
                )
                if last and g == 0:
                    nc.scalar.copy(result[:, g, :], acc)
                elif last:
                    nc.vector.tensor_copy(result[:, g, :], acc)
            if not last:
                nc.scalar.copy(result[:], shared[:])
            nc.sync.dma_start(out_rows[:, :, i * CHUNK : (i + 1) * CHUNK], result[:])

        for t in range(PACK):
            scatter(pa[t], a_lists, every, a_parts[t])
            for h in range(2):
                cols = slice(h * C // 2, (h + 1) * C // 2)
                nc.vector.tensor_tensor(rounded[h][:, t, :], pa[t][:, cols], gates[:, t, cols], ALU.mult)
            if t == 1:
                for i in range(CHUNKS):
                    weave(i, 0, nc.vector.tensor_copy)
        for i in range(CHUNKS + 1):
            if i < CHUNKS:
                weave(i, 2, nc.scalar.copy if i % 2 else nc.vector.tensor_copy)
            if i > 0:
                second_stage(i - 1)
